import numpy as np
import ml_dtypes


def mxq(x, axis, fmt="e4m3"):
    dtype, down = {"e4m3": (ml_dtypes.float8_e4m3fn, 7), "e5m2": (ml_dtypes.float8_e5m2, 14)}[fmt]
    v = np.moveaxis(np.asarray(x, np.float32).astype(ml_dtypes.bfloat16).astype(np.float64), axis, -1)
    blocks = v.reshape(v.shape[:-1] + (-1, 32))
    amax = np.abs(blocks).max(-1, keepdims=True)
    byte = np.maximum(np.where(amax > 0, np.frexp(amax)[1] - 1 + 127, 0) - down, 1)
    scale = np.exp2(byte - 127.0)
    codes = (blocks / scale).astype(np.float32).astype(dtype).astype(np.float64)
    return np.moveaxis((codes * scale).reshape(v.shape), -1, axis)


WIDE = False


def mx_kscale(k):
    if not WIDE:
        return np.ones(k)
    levels = np.array([10, -10, 5, -5, 0])
    if k % 512:
        return np.exp2(np.random.permutation(np.resize(levels, k // 32))).repeat(32)
    a = np.empty((k // 512, 16))
    for p in range(k // 512):
        a[p, :8] = np.random.permutation(np.resize(levels, 8))
        for g in range(8):
            far = levels[np.abs(levels - a[p, g]) >= 10]
            a[p, g + 8] = far[np.random.randint(len(far))]
    return np.exp2(a.ravel()).repeat(32)


BF16 = ml_dtypes.bfloat16


def bf(x):
    return np.asarray(x, np.float32).astype(BF16)


def f64(x):
    return np.asarray(x).astype(np.float64)


E2M1 = np.array([0.0, 0.5, 1.0, 1.5, 2.0, 3.0, 4.0, 6.0, -0.0, -0.5, -1.0, -1.5, -2.0, -3.0, -4.0, -6.0])


def pack_weight(w, fmt):
    k, n = w.shape
    w = f64(bf(w)).reshape(k // 32, 32, n)
    amax = np.abs(w).max(1)
    if fmt == "e4m3":
        byte = np.frexp(amax)[1] - 1 + 127 - 7
    else:
        mant, ex = np.frexp(amax / 6.0)
        byte = np.where(mant > 0.5, ex, ex - 1) + 127
    byte = np.clip(np.where(amax > 0, byte, 1), 1, 254)
    scaled = (w * np.exp2(127.0 - byte)[:, None, :]).reshape(k, n).astype(np.float32)
    by_word = np.ascontiguousarray(scaled.reshape(k // 512, 128, 4, n).transpose(0, 1, 3, 2))
    if fmt == "e4m3":
        words = by_word.astype(ml_dtypes.float8_e4m3fn).view(np.uint8)
    else:
        c = by_word.astype(ml_dtypes.float4_e2m1fn).view(np.uint8) & 0xF
        words = c[..., 0::2] | (c[..., 1::2] << 4)
    return np.ascontiguousarray(words), np.ascontiguousarray(byte.astype(np.uint8).reshape(k // 512, 16, n))


def unpack_weight(words, scales, fmt):
    g, p, n, _ = words.shape
    if fmt == "e4m3":
        vals = np.ascontiguousarray(words).view(ml_dtypes.float8_e4m3fn).astype(np.float64)
    else:
        nib = np.empty((g, p, n, 4), np.uint8)
        nib[..., 0::2] = words & 0xF
        nib[..., 1::2] = words >> 4
        vals = E2M1[nib]
    vals = vals * np.repeat(np.exp2(scales.astype(np.float64) - 127.0), 8, axis=1)[..., None]
    return vals.transpose(0, 1, 3, 2).reshape(g * 512, n)
def pack4(w):
    words, scales = pack_weight(w, "e2m1")
    return words.reshape(words.shape[0], 128, -1), scales


def unpack4(words, scales):
    return unpack_weight(words.reshape(words.shape[0], 128, -1, 2), scales, "e2m1")


M, D, N, R = 512, 1024, 4096, 1024


def setup_inputs():
    s = mx_kscale(D)
    t = mx_kscale(N)
    queries = np.random.standard_normal((D, M)) * s[:, None]
    keys = np.random.standard_normal((D, N)) / np.sqrt(D) / s[:, None] * t
    values = np.random.standard_normal((N, R)) / np.sqrt(N) / t[:, None]
    query_words, query_scales = pack4(queries)
    key_words, key_scales = pack4(keys)
    value_words, value_scales = pack_weight(values, "e4m3")
    return {"query_words": query_words, "query_scales": query_scales,
            "key_words": key_words, "key_scales": key_scales,
            "corr": bf(0.5 * np.random.standard_normal(N) * t),
            "value_words": value_words, "value_scales": value_scales}


def reference(query_words, query_scales, key_words, key_scales, corr, value_words, value_scales):
    qf = unpack4(query_words, query_scales)
    kc = unpack4(key_words, key_scales)
    v = unpack_weight(value_words, value_scales, "e4m3")
    scores = qf.T @ kc
    p = np.maximum(scores + f64(corr)[None, :], 0.0)
    return mxq(p, 1, "e4m3") @ v

@@ -1,0 +1,217 @@
+from contextlib import ExitStack
+
+import concourse.mybir as mybir
+
+M, D, N, R = 512, 1024, 4096, 1024
+FLOPS = 2 * M * D * N + 2 * M * N * R
+
+F32 = mybir.dt.float32
+BF16 = mybir.dt.bfloat16
+I32 = mybir.dt.int32
+U32 = mybir.dt.uint32
+U8 = mybir.dt.uint8
+FP4X4 = mybir.dt.float4_e2m1fn_x4
+FP8X4 = mybir.dt.float8_e4m3fn_x4
+ACT = mybir.ActivationFunctionType
+
+P = 128
+SLOTS = 4
+PASS = P * SLOTS
+CH_PASSES = D // PASS
+GROUPS = N // PASS
+BANK = 512
+EARLY_TILES = 5
+SCORE_BANKS = 8 - EARLY_TILES
+LAG = 2
+FIRST_SCALE_GROUPS = 3
+
+
+def tile_fp4_key_cache_attention_s4_kernel(
+    tc, query_words, query_scales, key_words, key_scales, corr, value_words, value_scales, out
+):
+    nc = tc.nc
+    out_tiles = [(m, h * BANK, BANK) for m in range(M // P) for h in range(R // BANK)]
+    last_m, last_first, last_width = out_tiles.pop()
+    out_tiles.extend((last_m, last_first + i * last_width // 2, last_width // 2) for i in range(2))
+    early_tiles, late_tiles = out_tiles[:EARLY_TILES], out_tiles[EARLY_TILES:]
+
+    with ExitStack() as ctx:
+        keep = ctx.enter_context(tc.tile_pool(name="keep", bufs=1))
+        work = ctx.enter_context(tc.tile_pool(name="work", bufs=3))
+        psum = ctx.enter_context(tc.psum_pool(name="psum", bufs=1))
+        ctx.enter_context(tc.manual_schedule())
+
+        def kept(name, shape, dtype):
+            return keep.tile(shape, dtype, name=name, align_bytes=64)
+
+        q_codes = kept("q_codes", [P, CH_PASSES, 2 * M], U8)
+        q_scales = kept("q_scales", [P, CH_PASSES, M], U8)
+        bias = kept("bias", [P, GROUPS, SLOTS], BF16)
+        scale_spans = [(0, FIRST_SCALE_GROUPS), (FIRST_SCALE_GROUPS, GROUPS)]
+        k_scales_raw = [
+            kept("k_scales_raw%d" % i, [P, CH_PASSES, (b - a) * PASS], U8) for i, (a, b) in enumerate(scale_spans)
+        ]
+        k_codes_raw = [kept("k_codes_raw%d" % g, [P, CH_PASSES, 2 * PASS], U8) for g in range(GROUPS)]
+        k_codes = [kept("k_codes%d" % g, [P, SLOTS, CH_PASSES, 2 * P], U8) for g in range(GROUPS)]
+        k_scales = [kept("k_scales%d" % g, [P, SLOTS, CH_PASSES, P], U8) for g in range(GROUPS)]
+        v_codes = [kept("v_codes%d" % g, [P, R], U32) for g in range(GROUPS)]
+        v_scales = [kept("v_scales%d" % i, [P, R], U8) for i in range(GROUPS // 4)]
+        p_codes = [kept("p_codes%d" % g, [P, M], U32) for g in range(GROUPS)]
+        p_scales = [kept("p_scales%d" % g, [P, M], U8) for g in range(GROUPS)]
+        warm_in = kept("warm_in", [P, 1], F32)
+        warm_out = kept("warm_out", [P, 1], F32)
+
+        nc.vector.memset(k_scales_raw[0][:].bitcast(I32), 0)
+        nc.vector.memset(q_scales[:].bitcast(I32), 0)
+        nc.vector.memset(warm_in[:], 0.0)
+        nc.scalar.activation(out=warm_out[:], in_=warm_in[:], func=ACT.Relu)
+        nc.gpsimd.memset(v_scales[0][:].bitcast(I32), 0)
+        nc.gpsimd.memset(k_scales_raw[1][:].bitcast(I32), 0)
+        nc.gpsimd.memset(v_scales[1][:].bitcast(I32), 0)
+
+        def load_scale_rows(plane, rows):
+            for r in range(4):
+                nc.sync.dma_start(
+                    out=plane[r:P:32].bitcast(I32),
+                    in_=rows[:, r:16:4, :].bitcast(I32).rearrange("c q w -> q c w"),
+                )
+
+        def load_key_scales(i):
+            a, b = scale_spans[i]
+            load_scale_rows(k_scales_raw[i], key_scales[:, :, a * PASS : b * PASS])
+
+        def load_key_codes(g):
+            nc.sync.dma_start(
+                out=k_codes_raw[g][:].bitcast(I32),
+                in_=key_words[:, :, 2 * PASS * g : 2 * PASS * (g + 1)].bitcast(I32).rearrange("c p w -> p c w"),
+            )
+
+        def load_value_codes(g):
+            nc.sync.dma_start(
+                out=v_codes[g][:].bitcast(I32),
+                in_=value_words[g].rearrange("p n t -> p (n t)").bitcast(I32),
+            )
+
+        def load_value_scales(i):
+            for quad in range(4):
+                nc.sync.dma_start(
+                    out=v_scales[i][32 * quad : 32 * quad + 16, :].bitcast(I32),
+                    in_=value_scales[4 * i : 4 * i + 4, 4 * quad : 4 * quad + 4, :].bitcast(I32),
+                )
+
+        load_key_codes(0)
+        load_key_scales(0)
+        nc.sync.dma_start(out=q_codes[:].bitcast(I32), in_=query_words.bitcast(I32).rearrange("c p w -> p c w"))
+        load_scale_rows(q_scales, query_scales)
+        nc.sync.dma_start(out=bias[:], in_=corr.rearrange("(g p t) -> p g t", p=P, t=SLOTS))
+        load_key_codes(1)
+        load_key_codes(2)
+        load_key_scales(1)
+        load_value_scales(0)
+        for g in range(GROUPS):
+            if g + 3 < GROUPS:
+                load_key_codes(g + 3)
+            if g == 3:
+                load_value_scales(1)
+            load_value_codes(g)
+
+        def sort_key_codes(g, slots):
+            nc.vector.tensor_copy(
+                out=k_codes[g][:, slots].rearrange("p t c (m b) -> p t c m b", b=2),
+                in_=k_codes_raw[g][:].rearrange("p c (m t b) -> p t c m b", t=SLOTS, b=2)[:, slots],
+            )
+
+        def sort_key_scales(g, slots):
+            i = 0 if g < FIRST_SCALE_GROUPS else 1
+            first = (g - scale_spans[i][0]) * PASS
+            nc.vector.tensor_copy(
+                out=k_scales[g][:, slots],
+                in_=k_scales_raw[i][:, :, first : first + PASS].rearrange("p c (m t) -> p t c m", t=SLOTS)[:, slots],
+            )
+
+        relu = {}
+        grouped = {}
+
+        def scores(g):
+            relu[g] = work.tile([P, SLOTS, M], BF16, name="relu", align_bytes=64)
+            for t in range(SLOTS):
+                bank = psum.tile([P, BANK], F32, name="score_bank", tag="score", bufs=SCORE_BANKS)
+                for c in range(CH_PASSES):
+                    nc.tensor.matmul_mx(
+                        out=bank[:],
+                        lhsT=k_codes[g][:, t, c, :].bitcast(FP4X4),
+                        lhsT_scale=k_scales[g][:, t, c, :],
+                        rhs=q_codes[:, c, :].bitcast(FP4X4),
+                        rhs_scale=q_scales[:, c, :],
+                        start=(c == 0),
+                        stop=(c == CH_PASSES - 1),
+                    )
+                nc.scalar.activation(out=relu[g][:, t, :], in_=bank[:], func=ACT.Relu, bias=bias[:, g, t : t + 1])
+
+        def interleave(g):
+            grouped[g] = work.tile([P, M, SLOTS], BF16, name="grouped", align_bytes=64)
+            nc.vector.tensor_copy(
+                out=grouped[g][:].rearrange("p (c i) t -> p c t i", i=4),
+                in_=relu[g][:].rearrange("p t (c i) -> p c t i", i=4),
+            )
+
+        def quantize(g):
+            nc.vector.quantize_mx(
+                out=p_codes[g][:].bitcast(FP8X4),
+                scales=p_scales[g][:],
+                in_=grouped[g][:].rearrange("p m t -> p (m t)"),
+            )
+
+        def value_pass(bank, tile_at, g):
+            m, first, width = tile_at
+            queries = slice(m * P, (m + 1) * P)
+            channels = slice(first, first + width)
+            nc.tensor.matmul_mx(
+                out=bank[:, :width],
+                lhsT=p_codes[g][:, queries].bitcast(FP8X4),
+                lhsT_scale=p_scales[g][:, queries],
+                rhs=v_codes[g][:, channels].bitcast(FP8X4),
+                rhs_scale=v_scales[g // 4][4 * (g % 4) :, channels],
+                start=(g == 0),
+                stop=(g == GROUPS - 1),
+            )
+
+        def store(bank, tile_at, on_scalar):
+            m, first, width = tile_at
+            result = keep.tile([P, width], F32, name="result%d_%d" % (m, first))
+            if on_scalar:
+                nc.scalar.copy(out=result[:], in_=bank[:, :width])
+            else:
+                nc.vector.tensor_copy(out=result[:], in_=bank[:, :width])
+            nc.sync.dma_start(out=out[m * P : (m + 1) * P, first : first + width], in_=result[:])
+
+        early_banks = [psum.tile([P, BANK], F32, name="early%d" % i) for i in range(EARLY_TILES)]
+
+        every_slot = slice(0, SLOTS)
+        for slots in (slice(0, 2), slice(2, 4)):
+            sort_key_codes(0, slots)
+            sort_key_scales(0, slots)
+        for g in range(1, LAG + 1):
+            sort_key_codes(g, every_slot)
+            sort_key_scales(g, every_slot)
+        for g in range(LAG):
+            scores(g)
+        for g in range(GROUPS):
+            ahead = g + LAG + 1
+            interleave(g)
+            if ahead < GROUPS:
+                sort_key_codes(ahead, every_slot)
+            quantize(g)
+            if ahead < GROUPS:
+                sort_key_scales(ahead, every_slot)
+            if g + LAG < GROUPS:
+                scores(g + LAG)
+            for bank, tile_at in zip(early_banks, early_tiles):
+                value_pass(bank, tile_at, g)
+        for i, (bank, tile_at) in enumerate(zip(early_banks, early_tiles)):
+            store(bank, tile_at, i % 2 == 0)
+        for i, tile_at in enumerate(late_tiles):
+            bank = psum.tile([P, BANK], F32, name="late_bank", tag="score", bufs=SCORE_BANKS)
+            for g in range(GROUPS):
+                value_pass(bank, tile_at, g)
+            store(bank, tile_at, i % 2 == 0)

@@ -20,10 +20,14 @@ PASS = P * SLOTS
 CH_PASSES = D // PASS
 GROUPS = N // PASS
 BANK = 512
-EARLY_TILES = 5
-SCORE_BANKS = 8 - EARLY_TILES
-LAG = 2
-FIRST_SCALE_GROUPS = 3
+BANKS = 8
+ROUNDS = 5
+FIRST_SHARED = 2
+KEY_CODE_SPANS = [(0, 1), (1, 3), (3, 5), (5, 8)]
+KEY_SCALE_SPANS = [(0, 1), (1, 4), (4, 8)]
+BIAS_SPANS = [(0, 2), (2, 8)]
+BIAS_ROW = 16
+SCALAR_QUERIES = 224
 
 
 def tile_fp4_key_cache_attention_s4_kernel(
@@ -33,12 +37,10 @@ def tile_fp4_key_cache_attention_s4_kernel(
     out_tiles = [(m, h * BANK, BANK) for m in range(M // P) for h in range(R // BANK)]
     last_m, last_first, last_width = out_tiles.pop()
     out_tiles.extend((last_m, last_first + i * last_width // 2, last_width // 2) for i in range(2))
-    early_tiles, late_tiles = out_tiles[:EARLY_TILES], out_tiles[EARLY_TILES:]
 
     with ExitStack() as ctx:
         keep = ctx.enter_context(tc.tile_pool(name="keep", bufs=1))
-        work = ctx.enter_context(tc.tile_pool(name="work", bufs=3))
-        psum = ctx.enter_context(tc.psum_pool(name="psum", bufs=1))
+        psum = ctx.enter_context(tc.psum_pool(name="psum", bufs=BANKS))
         ctx.enter_context(tc.manual_schedule())
 
         def kept(name, shape, dtype):
@@ -46,14 +48,16 @@ def tile_fp4_key_cache_attention_s4_kernel(
 
         q_codes = kept("q_codes", [P, CH_PASSES, 2 * M], U8)
         q_scales = kept("q_scales", [P, CH_PASSES, M], U8)
-        bias = kept("bias", [P, GROUPS, SLOTS], BF16)
-        scale_spans = [(0, FIRST_SCALE_GROUPS), (FIRST_SCALE_GROUPS, GROUPS)]
-        k_scales_raw = [
-            kept("k_scales_raw%d" % i, [P, CH_PASSES, (b - a) * PASS], U8) for i, (a, b) in enumerate(scale_spans)
-        ]
-        k_codes_raw = [kept("k_codes_raw%d" % g, [P, CH_PASSES, 2 * PASS], U8) for g in range(GROUPS)]
-        k_codes = [kept("k_codes%d" % g, [P, SLOTS, CH_PASSES, 2 * P], U8) for g in range(GROUPS)]
-        k_scales = [kept("k_scales%d" % g, [P, SLOTS, CH_PASSES, P], U8) for g in range(GROUPS)]
+        bias = [kept("bias%d" % a, [P, b - a, BIAS_ROW], BF16) for a, b in BIAS_SPANS]
+        k_scales_raw = [kept("k_scales_raw%d" % a, [P, CH_PASSES, (b - a) * PASS], U8) for a, b in KEY_SCALE_SPANS]
+        k_codes_raw = [kept("k_codes_raw%d" % a, [P, CH_PASSES, (b - a) * 2 * PASS], U8) for a, b in KEY_CODE_SPANS]
+
+        def span_of(spans, g):
+            i = max(j for j, (a, b) in enumerate(spans) if a <= g)
+            return i, g - spans[i][0]
+
+        k_codes = [kept("k_codes%d" % g, [P, CH_PASSES, SLOTS, 2 * P], U8) for g in range(GROUPS)]
+        k_scales = [kept("k_scales%d" % g, [P, CH_PASSES, SLOTS, P], U8) for g in range(GROUPS)]
         v_codes = [kept("v_codes%d" % g, [P, R], U32) for g in range(GROUPS)]
         v_scales = [kept("v_scales%d" % i, [P, R], U8) for i in range(GROUPS // 4)]
         p_codes = [kept("p_codes%d" % g, [P, M], U32) for g in range(GROUPS)]
@@ -65,9 +69,10 @@ def tile_fp4_key_cache_attention_s4_kernel(
         nc.vector.memset(q_scales[:].bitcast(I32), 0)
         nc.vector.memset(warm_in[:], 0.0)
         nc.scalar.activation(out=warm_out[:], in_=warm_in[:], func=ACT.Relu)
-        nc.gpsimd.memset(v_scales[0][:].bitcast(I32), 0)
-        nc.gpsimd.memset(k_scales_raw[1][:].bitcast(I32), 0)
-        nc.gpsimd.memset(v_scales[1][:].bitcast(I32), 0)
+        nc.vector.memset(k_scales_raw[1][:].bitcast(I32), 0)
+        nc.vector.memset(v_scales[0][:].bitcast(I32), 0)
+        nc.vector.memset(k_scales_raw[2][:].bitcast(I32), 0)
+        nc.vector.memset(v_scales[1][:].bitcast(I32), 0)
 
         def load_scale_rows(plane, rows):
             for r in range(4):
@@ -77,13 +82,21 @@ def tile_fp4_key_cache_attention_s4_kernel(
                 )
 
         def load_key_scales(i):
-            a, b = scale_spans[i]
+            a, b = KEY_SCALE_SPANS[i]
             load_scale_rows(k_scales_raw[i], key_scales[:, :, a * PASS : b * PASS])
 
-        def load_key_codes(g):
+        def load_key_codes(i):
+            a, b = KEY_CODE_SPANS[i]
             nc.sync.dma_start(
-                out=k_codes_raw[g][:].bitcast(I32),
-                in_=key_words[:, :, 2 * PASS * g : 2 * PASS * (g + 1)].bitcast(I32).rearrange("c p w -> p c w"),
+                out=k_codes_raw[i][:].bitcast(I32),
+                in_=key_words[:, :, 2 * PASS * a : 2 * PASS * b].bitcast(I32).rearrange("c p w -> p c w"),
+            )
+
+        def load_bias(i):
+            a, b = BIAS_SPANS[i]
+            nc.sync.dma_start(
+                out=bias[i][:, :, :SLOTS],
+                in_=corr[a * PASS : b * PASS].rearrange("(g p t) -> p g t", p=P, t=SLOTS),
             )
 
         def load_value_codes(g):
@@ -103,57 +116,61 @@ def tile_fp4_key_cache_attention_s4_kernel(
         load_key_scales(0)
         nc.sync.dma_start(out=q_codes[:].bitcast(I32), in_=query_words.bitcast(I32).rearrange("c p w -> p c w"))
         load_scale_rows(q_scales, query_scales)
-        nc.sync.dma_start(out=bias[:], in_=corr.rearrange("(g p t) -> p g t", p=P, t=SLOTS))
+        load_bias(0)
         load_key_codes(1)
-        load_key_codes(2)
         load_key_scales(1)
+        load_key_codes(2)
+        load_bias(1)
+        load_key_scales(2)
+        load_key_codes(3)
         load_value_scales(0)
+        load_value_scales(1)
         for g in range(GROUPS):
-            if g + 3 < GROUPS:
-                load_key_codes(g + 3)
-            if g == 3:
-                load_value_scales(1)
             load_value_codes(g)
 
         def sort_key_codes(g, slots):
+            i, at = span_of(KEY_CODE_SPANS, g)
+            raw = k_codes_raw[i][:, :, at * 2 * PASS : (at + 1) * 2 * PASS]
             nc.vector.tensor_copy(
-                out=k_codes[g][:, slots].rearrange("p t c (m b) -> p t c m b", b=2),
-                in_=k_codes_raw[g][:].rearrange("p c (m t b) -> p t c m b", t=SLOTS, b=2)[:, slots],
+                out=k_codes[g][:, :, slots].rearrange("p c t (m b) -> p c t m b", b=2),
+                in_=raw.rearrange("p c (m t b) -> p c t m b", t=SLOTS, b=2)[:, :, slots],
             )
 
         def sort_key_scales(g, slots):
-            i = 0 if g < FIRST_SCALE_GROUPS else 1
-            first = (g - scale_spans[i][0]) * PASS
+            i, at = span_of(KEY_SCALE_SPANS, g)
+            raw = k_scales_raw[i][:, :, at * PASS : (at + 1) * PASS]
             nc.vector.tensor_copy(
-                out=k_scales[g][:, slots],
-                in_=k_scales_raw[i][:, :, first : first + PASS].rearrange("p c (m t) -> p t c m", t=SLOTS)[:, slots],
+                out=k_scales[g][:, :, slots],
+                in_=raw.rearrange("p c (m t) -> p c t m", t=SLOTS)[:, :, slots],
             )
 
-        relu = {}
-        grouped = {}
+        relu = [kept("relu%d" % g, [P, SLOTS, M], BF16) for g in range(GROUPS)]
+        grouped = [kept("grouped%d" % g, [P, M, SLOTS], BF16) for g in range(GROUPS)]
 
-        def scores(g):
-            relu[g] = work.tile([P, SLOTS, M], BF16, name="relu", align_bytes=64)
-            for t in range(SLOTS):
-                bank = psum.tile([P, BANK], F32, name="score_bank", tag="score", bufs=SCORE_BANKS)
+        def scores(g, slots):
+            i, at = span_of(BIAS_SPANS, g)
+            for t in range(slots.start, slots.stop):
+                bank = psum.tile([P, BANK], F32, name="score_bank", tag="bank")
                 for c in range(CH_PASSES):
                     nc.tensor.matmul_mx(
                         out=bank[:],
-                        lhsT=k_codes[g][:, t, c, :].bitcast(FP4X4),
-                        lhsT_scale=k_scales[g][:, t, c, :],
+                        lhsT=k_codes[g][:, c, t, :].bitcast(FP4X4),
+                        lhsT_scale=k_scales[g][:, c, t, :],
                         rhs=q_codes[:, c, :].bitcast(FP4X4),
                         rhs_scale=q_scales[:, c, :],
                         start=(c == 0),
                         stop=(c == CH_PASSES - 1),
                     )
-                nc.scalar.activation(out=relu[g][:, t, :], in_=bank[:], func=ACT.Relu, bias=bias[:, g, t : t + 1])
+                nc.scalar.activation(out=relu[g][:, t, :], in_=bank[:], func=ACT.Relu, bias=bias[i][:, at, t : t + 1])
+
+        def interleaving(g, queries):
+            return dict(
+                out=grouped[g][:, queries, :].rearrange("p (c i) t -> p c t i", i=4),
+                in_=relu[g][:, :, queries].rearrange("p t (c i) -> p c t i", i=4),
+            )
 
         def interleave(g):
-            grouped[g] = work.tile([P, M, SLOTS], BF16, name="grouped", align_bytes=64)
-            nc.vector.tensor_copy(
-                out=grouped[g][:].rearrange("p (c i) t -> p c t i", i=4),
-                in_=relu[g][:].rearrange("p t (c i) -> p c t i", i=4),
-            )
+            nc.vector.tensor_copy(**interleaving(g, slice(SCALAR_QUERIES if g >= FIRST_SHARED else 0, M)))
 
         def quantize(g):
             nc.vector.quantize_mx(
@@ -185,33 +202,32 @@ def tile_fp4_key_cache_attention_s4_kernel(
                 nc.vector.tensor_copy(out=result[:], in_=bank[:, :width])
             nc.sync.dma_start(out=out[m * P : (m + 1) * P, first : first + width], in_=result[:])
 
-        early_banks = [psum.tile([P, BANK], F32, name="early%d" % i) for i in range(EARLY_TILES)]
-
-        every_slot = slice(0, SLOTS)
-        for slots in (slice(0, 2), slice(2, 4)):
-            sort_key_codes(0, slots)
-            sort_key_scales(0, slots)
-        for g in range(1, LAG + 1):
-            sort_key_codes(g, every_slot)
-            sort_key_scales(g, every_slot)
-        for g in range(LAG):
-            scores(g)
         for g in range(GROUPS):
-            ahead = g + LAG + 1
-            interleave(g)
-            if ahead < GROUPS:
-                sort_key_codes(ahead, every_slot)
+            for slots in (slice(0, 2), slice(2, 4)):
+                if g == GROUPS - 1 and slots.start > 0:
+                    interleave(0)
+                sort_key_codes(g, slots)
+                sort_key_scales(g, slots)
+                scores(g, slots)
+
+        for g in range(FIRST_SHARED, GROUPS):
+            nc.scalar.copy(**interleaving(g, slice(0, SCALAR_QUERIES)))
+        quantize(0)
+        interleave(1)
+        for g in range(1, GROUPS):
+            if g + 1 < GROUPS:
+                interleave(g + 1)
             quantize(g)
-            if ahead < GROUPS:
-                sort_key_scales(ahead, every_slot)
-            if g + LAG < GROUPS:
-                scores(g + LAG)
-            for bank, tile_at in zip(early_banks, early_tiles):
+
+        banks = [psum.tile([P, BANK], F32, name="out_bank%d" % i, tag="bank") for i in range(BANKS)]
+        for g in range(ROUNDS):
+            for bank, tile_at in zip(banks, out_tiles):
                 value_pass(bank, tile_at, g)
-        for i, (bank, tile_at) in enumerate(zip(early_banks, early_tiles)):
-            store(bank, tile_at, i % 2 == 0)
-        for i, tile_at in enumerate(late_tiles):
-            bank = psum.tile([P, BANK], F32, name="late_bank", tag="score", bufs=SCORE_BANKS)
-            for g in range(GROUPS):
+        for i, (bank, tile_at) in enumerate(zip(banks, out_tiles)):
+            for g in range(ROUNDS, GROUPS):
                 value_pass(bank, tile_at, g)
             store(bank, tile_at, i % 2 == 0)
+        last_bank = psum.tile([P, BANK], F32, name="last_bank", tag="bank")
+        for g in range(GROUPS):
+            value_pass(last_bank, out_tiles[BANKS], g)
+        store(last_bank, out_tiles[BANKS], True)

from contextlib import ExitStack

import concourse.mybir as mybir

M, D, N, R = 512, 1024, 4096, 1024
FLOPS = 2 * M * D * N + 2 * M * N * R

F32 = mybir.dt.float32
BF16 = mybir.dt.bfloat16
I32 = mybir.dt.int32
U32 = mybir.dt.uint32
U8 = mybir.dt.uint8
FP4X4 = mybir.dt.float4_e2m1fn_x4
FP8X4 = mybir.dt.float8_e4m3fn_x4
ACT = mybir.ActivationFunctionType

P = 128
SLOTS = 4
PASS = P * SLOTS
CH_PASSES = D // PASS
GROUPS = N // PASS
BANK = 512
BANKS = 8
ROUNDS = 5
FIRST_SHARED = 2
KEY_CODE_SPANS = [(0, 1), (1, 3), (3, 5), (5, 8)]
KEY_SCALE_SPANS = [(0, 1), (1, 4), (4, 8)]
BIAS_SPANS = [(0, 2), (2, 8)]
BIAS_ROW = 16
SCALAR_QUERIES = 224


def tile_fp4_key_cache_attention_s4_kernel(
    tc, query_words, query_scales, key_words, key_scales, corr, value_words, value_scales, out
):
    nc = tc.nc
    out_tiles = [(m, h * BANK, BANK) for m in range(M // P) for h in range(R // BANK)]
    last_m, last_first, last_width = out_tiles.pop()
    out_tiles.extend((last_m, last_first + i * last_width // 2, last_width // 2) for i in range(2))

    with ExitStack() as ctx:
        keep = ctx.enter_context(tc.tile_pool(name="keep", bufs=1))
        psum = ctx.enter_context(tc.psum_pool(name="psum", bufs=BANKS))
        ctx.enter_context(tc.manual_schedule())

        def kept(name, shape, dtype):
            return keep.tile(shape, dtype, name=name, align_bytes=64)

        q_codes = kept("q_codes", [P, CH_PASSES, 2 * M], U8)
        q_scales = kept("q_scales", [P, CH_PASSES, M], U8)
        bias = [kept("bias%d" % a, [P, b - a, BIAS_ROW], BF16) for a, b in BIAS_SPANS]
        k_scales_raw = [kept("k_scales_raw%d" % a, [P, CH_PASSES, (b - a) * PASS], U8) for a, b in KEY_SCALE_SPANS]
        k_codes_raw = [kept("k_codes_raw%d" % a, [P, CH_PASSES, (b - a) * 2 * PASS], U8) for a, b in KEY_CODE_SPANS]

        def span_of(spans, g):
            i = max(j for j, (a, b) in enumerate(spans) if a <= g)
            return i, g - spans[i][0]

        k_codes = [kept("k_codes%d" % g, [P, CH_PASSES, SLOTS, 2 * P], U8) for g in range(GROUPS)]
        k_scales = [kept("k_scales%d" % g, [P, CH_PASSES, SLOTS, P], U8) for g in range(GROUPS)]
        v_codes = [kept("v_codes%d" % g, [P, R], U32) for g in range(GROUPS)]
        v_scales = [kept("v_scales%d" % i, [P, R], U8) for i in range(GROUPS // 4)]
        p_codes = [kept("p_codes%d" % g, [P, M], U32) for g in range(GROUPS)]
        p_scales = [kept("p_scales%d" % g, [P, M], U8) for g in range(GROUPS)]
        warm_in = kept("warm_in", [P, 1], F32)
        warm_out = kept("warm_out", [P, 1], F32)

        nc.vector.memset(k_scales_raw[0][:].bitcast(I32), 0)
        nc.vector.memset(q_scales[:].bitcast(I32), 0)
        nc.vector.memset(warm_in[:], 0.0)
        nc.scalar.activation(out=warm_out[:], in_=warm_in[:], func=ACT.Relu)
        nc.vector.memset(k_scales_raw[1][:].bitcast(I32), 0)
        nc.vector.memset(v_scales[0][:].bitcast(I32), 0)
        nc.vector.memset(k_scales_raw[2][:].bitcast(I32), 0)
        nc.vector.memset(v_scales[1][:].bitcast(I32), 0)

        def load_scale_rows(plane, rows):
            for r in range(4):
                nc.sync.dma_start(
                    out=plane[r:P:32].bitcast(I32),
                    in_=rows[:, r:16:4, :].bitcast(I32).rearrange("c q w -> q c w"),
                )

        def load_key_scales(i):
            a, b = KEY_SCALE_SPANS[i]
            load_scale_rows(k_scales_raw[i], key_scales[:, :, a * PASS : b * PASS])

        def load_key_codes(i):
            a, b = KEY_CODE_SPANS[i]
            nc.sync.dma_start(
                out=k_codes_raw[i][:].bitcast(I32),
                in_=key_words[:, :, 2 * PASS * a : 2 * PASS * b].bitcast(I32).rearrange("c p w -> p c w"),
            )

        def load_bias(i):
            a, b = BIAS_SPANS[i]
            nc.sync.dma_start(
                out=bias[i][:, :, :SLOTS],
                in_=corr[a * PASS : b * PASS].rearrange("(g p t) -> p g t", p=P, t=SLOTS),
            )

        def load_value_codes(g):
            nc.sync.dma_start(
                out=v_codes[g][:].bitcast(I32),
                in_=value_words[g].rearrange("p n t -> p (n t)").bitcast(I32),
            )

        def load_value_scales(i):
            for quad in range(4):
                nc.sync.dma_start(
                    out=v_scales[i][32 * quad : 32 * quad + 16, :].bitcast(I32),
                    in_=value_scales[4 * i : 4 * i + 4, 4 * quad : 4 * quad + 4, :].bitcast(I32),
                )

        load_key_codes(0)
        load_key_scales(0)
        nc.sync.dma_start(out=q_codes[:].bitcast(I32), in_=query_words.bitcast(I32).rearrange("c p w -> p c w"))
        load_scale_rows(q_scales, query_scales)
        load_bias(0)
        load_key_codes(1)
        load_key_scales(1)
        load_key_codes(2)
        load_bias(1)
        load_key_scales(2)
        load_key_codes(3)
        load_value_scales(0)
        load_value_scales(1)
        for g in range(GROUPS):
            load_value_codes(g)

        def sort_key_codes(g, slots):
            i, at = span_of(KEY_CODE_SPANS, g)
            raw = k_codes_raw[i][:, :, at * 2 * PASS : (at + 1) * 2 * PASS]
            nc.vector.tensor_copy(
                out=k_codes[g][:, :, slots].rearrange("p c t (m b) -> p c t m b", b=2),
                in_=raw.rearrange("p c (m t b) -> p c t m b", t=SLOTS, b=2)[:, :, slots],
            )

        def sort_key_scales(g, slots):
            i, at = span_of(KEY_SCALE_SPANS, g)
            raw = k_scales_raw[i][:, :, at * PASS : (at + 1) * PASS]
            nc.vector.tensor_copy(
                out=k_scales[g][:, :, slots],
                in_=raw.rearrange("p c (m t) -> p c t m", t=SLOTS)[:, :, slots],
            )

        relu = [kept("relu%d" % g, [P, SLOTS, M], BF16) for g in range(GROUPS)]
        grouped = [kept("grouped%d" % g, [P, M, SLOTS], BF16) for g in range(GROUPS)]

        def scores(g, slots):
            i, at = span_of(BIAS_SPANS, g)
            for t in range(slots.start, slots.stop):
                bank = psum.tile([P, BANK], F32, name="score_bank", tag="bank")
                for c in range(CH_PASSES):
                    nc.tensor.matmul_mx(
                        out=bank[:],
                        lhsT=k_codes[g][:, c, t, :].bitcast(FP4X4),
                        lhsT_scale=k_scales[g][:, c, t, :],
                        rhs=q_codes[:, c, :].bitcast(FP4X4),
                        rhs_scale=q_scales[:, c, :],
                        start=(c == 0),
                        stop=(c == CH_PASSES - 1),
                    )
                nc.scalar.activation(out=relu[g][:, t, :], in_=bank[:], func=ACT.Relu, bias=bias[i][:, at, t : t + 1])

        def interleaving(g, queries):
            return dict(
                out=grouped[g][:, queries, :].rearrange("p (c i) t -> p c t i", i=4),
                in_=relu[g][:, :, queries].rearrange("p t (c i) -> p c t i", i=4),
            )

        def interleave(g):
            nc.vector.tensor_copy(**interleaving(g, slice(SCALAR_QUERIES if g >= FIRST_SHARED else 0, M)))

        def quantize(g):
            nc.vector.quantize_mx(
                out=p_codes[g][:].bitcast(FP8X4),
                scales=p_scales[g][:],
                in_=grouped[g][:].rearrange("p m t -> p (m t)"),
            )

        def value_pass(bank, tile_at, g):
            m, first, width = tile_at
            queries = slice(m * P, (m + 1) * P)
            channels = slice(first, first + width)
            nc.tensor.matmul_mx(
                out=bank[:, :width],
                lhsT=p_codes[g][:, queries].bitcast(FP8X4),
                lhsT_scale=p_scales[g][:, queries],
                rhs=v_codes[g][:, channels].bitcast(FP8X4),
                rhs_scale=v_scales[g // 4][4 * (g % 4) :, channels],
                start=(g == 0),
                stop=(g == GROUPS - 1),
            )

        def store(bank, tile_at, on_scalar):
            m, first, width = tile_at
            result = keep.tile([P, width], F32, name="result%d_%d" % (m, first))
            if on_scalar:
                nc.scalar.copy(out=result[:], in_=bank[:, :width])
            else:
                nc.vector.tensor_copy(out=result[:], in_=bank[:, :width])
            nc.sync.dma_start(out=out[m * P : (m + 1) * P, first : first + width], in_=result[:])

        for g in range(GROUPS):
            for slots in (slice(0, 2), slice(2, 4)):
                if g == GROUPS - 1 and slots.start > 0:
                    interleave(0)
                sort_key_codes(g, slots)
                sort_key_scales(g, slots)
                scores(g, slots)

        for g in range(FIRST_SHARED, GROUPS):
            nc.scalar.copy(**interleaving(g, slice(0, SCALAR_QUERIES)))
        quantize(0)
        interleave(1)
        for g in range(1, GROUPS):
            if g + 1 < GROUPS:
                interleave(g + 1)
            quantize(g)

        banks = [psum.tile([P, BANK], F32, name="out_bank%d" % i, tag="bank") for i in range(BANKS)]
        for g in range(ROUNDS):
            for bank, tile_at in zip(banks, out_tiles):
                value_pass(bank, tile_at, g)
        for i, (bank, tile_at) in enumerate(zip(banks, out_tiles)):
            for g in range(ROUNDS, GROUPS):
                value_pass(bank, tile_at, g)
            store(bank, tile_at, i % 2 == 0)
        last_bank = psum.tile([P, BANK], F32, name="last_bank", tag="bank")
        for g in range(GROUPS):
            value_pass(last_bank, out_tiles[BANKS], g)
        store(last_bank, out_tiles[BANKS], True)
